import numpy as np, ml_dtypes
CORES = [31,71,111]
N = 3
import mx_ref
NC, G = 128, 2
C = np.float32(0.037)
BF = ml_dtypes.bfloat16
def cut(t, i, w=512):
    return t[:, w * i:w * i + w]
def tile(rs):
    return np.stack(rs, axis=2).reshape(128, -1).astype(BF)
def layer(w, X):
    out = []
    for i in range(G):
        for t in range(len(X)):
            p = mx_ref.matmul(mx_ref.quantize(cut(w, len(X) * i + t)), X[t])
            z = p if t == 0 else z + p
        out.append(z)
    return out
def act(Z):
    return [np.maximum(s * z, 0) * C for z in Z for s in (1, -1)]
def pick(b):
    s = np.zeros((128, 128, 4), np.float32)
    s[np.arange(128), np.arange(128), b] = 1.0
    return mx_ref.quantize(s.reshape(128, 512).astype(BF))
def setup_inputs(rng):
    def f(*shape):
        return mx_ref.flush((rng.standard_normal(shape, dtype=np.float32) * np.exp2(rng.integers(-2, 3, shape[:-1] + (1,)))).astype(BF))
    return {"a": f(N, 128, G * 512), "b": f(N, 128, N * 4 * NC)}
def setup_inputs_blocks(rng):
    d = setup_inputs(rng)
    for k in ("a", "b"): d[k] = mx_ref.spread(d[k], rng, 4)
    return d
def setup_inputs_wide(rng):
    d = setup_inputs(rng)
    for k in ("a", "b"): d[k] = mx_ref.flush((d[k].astype(np.float32) * np.exp2(rng.integers(-8, 9, (N, 1, 1))).astype(np.float32)).astype(BF))
    return d
def reference(a, b):
    S = [pick(t) for t in range(4)]
    y = np.zeros((N, 128, NC, 4), np.float32)
    for c in range(N):
        for r in range(N):
            q = mx_ref.quantize(tile(act(layer(a[r], [mx_ref.quantize(cut(b[r], c, 4 * NC))]))))
            p = np.stack([mx_ref.matmul(S[t], q) for t in range(4)], axis=2)
            y[c] = p if r == 0 else y[c] + p
    return {"y": y.reshape(N, 128, 4 * NC)}

@@ -1,0 +1,144 @@
+from concourse.mybir import dt, AluOpType, ActivationFunctionType
+
+C = 0.037
+W = 512
+NC = 128
+
+SCRATCH = {
+    "at": ("sbuf", [128, 2 * W], "bfloat16"),
+    "bt": ("sbuf", [128, 3 * W], "bfloat16"),
+    "qa": ("sbuf", [128, 2 * NC], "float8_e4m3fn_x4"),
+    "sa": ("sbuf", [128, 2 * NC], "uint8"),
+    "qb": ("sbuf", [128, 3 * NC], "float8_e4m3fn_x4"),
+    "sb": ("sbuf", [128, 3 * NC], "uint8"),
+    "gt": ("sbuf", [128, 3 * W], "bfloat16"),
+    "qg": ("sbuf", [128, 3 * NC], "float8_e4m3fn_x4"),
+    "sg": ("sbuf", [128, 3 * NC], "uint8"),
+    "strip": ("sbuf", [128, W + 4], "bfloat16"),
+    "qs": ("sbuf", [128, 4 * NC], "float8_e4m3fn_x4"),
+    "ss": ("sbuf", [128, 4 * NC], "uint8"),
+    "lq0": ("sbuf", [128, NC], "float8_e4m3fn_x4"),
+    "ls0": ("sbuf", [128, NC], "uint8"),
+    "lq1": ("sbuf", [128, NC], "float8_e4m3fn_x4"),
+    "ls1": ("sbuf", [128, NC], "uint8"),
+    "yt": ("sbuf", [128, W], "float32"),
+    "z": ("psum", [128, 4 * 512], "float32"),
+    "d": ("psum", [128, 4 * 512], "float32"),
+}
+SEMAPHORES = (["ld_a", "ones", "eye", "qa0", "qa1", "qs", "arr0", "arr1", "sent", "yr", "st"]
+              + ["%s%d" % (n, k) for n in ("ld_b", "qb", "z0_", "z1_", "av", "as", "qg") for k in range(3)]
+              + ["dd%d" % b for b in range(4)])
+
+
+def rank_program(g, core, T, topo):
+    rank = T.rank_of(core)
+    if rank is None:
+        return
+    n = len(T.cores)
+    S = T.sem
+    v, sc, te, sy = g.vector, g.scalar, g.tensor, g.sync
+    order = [(rank + 1) % n, (rank + 2) % n, rank]
+
+    def tcols(i):
+        return slice(W * i, W * i + W)
+
+    def qcols(i):
+        return slice(NC * i, NC * i + NC)
+
+    def bank(i):
+        return slice(512 * i, 512 * i + NC)
+
+    sy.dma_start(T.at[:, :], T.a[:, :]).then_inc(S.ld_a, 16)
+    sc.dma_start(T.bt[:, tcols(0)], T.b[:, tcols(order[0])]).then_inc(S.ld_b0, 16)
+    sy.dma_start(T.bt[:, tcols(1)], T.b[:, tcols(order[1])]).then_inc(S.ld_b1, 16)
+    sc.dma_start(T.bt[:, tcols(2)], T.b[:, tcols(order[2])]).then_inc(S.ld_b2, 16)
+
+    v.memset(T.strip[:, :], 1.0).then_inc(S.ones, 1)
+    g.wait_ge(S.ones, 1)
+    g.affine_select(T.strip[:, :], T.strip[:, :], [[1, W + 4]], AluOpType.is_equal, 0.0, -3, -4).then_inc(S.eye, 1)
+
+    v.wait_ge(S.ld_b0, 16)
+    v.quantize_mx(T.qb[:, qcols(0)], T.sb[:, qcols(0)], T.bt[:, tcols(0)]).then_inc(S.qb0, 1)
+    v.wait_ge(S.ld_a, 16)
+    for i in range(2):
+        v.quantize_mx(T.qa[:, qcols(i)], T.sa[:, qcols(i)], T.at[:, tcols(i)]).then_inc(S["qa%d" % i], 1)
+
+    zbank = [(0, 1), (2, 3), (0, 1)]
+
+    def col(k, b):
+        return slice(W * k + b, W * k + W, 4)
+
+    for k in range(3):
+        b0, b1 = zbank[k]
+        te.wait_ge(S["qb%d" % k], 1)
+        if k == 0:
+            te.wait_ge(S.qa0, 1)
+        if k == 2:
+            te.wait_ge(S.av0, 2)
+            te.wait_ge(S.as0, 2)
+        te.matmul_mx(T.z[:, bank(b0)], T.qa[:, qcols(0)], T.sa[:, qcols(0)],
+                     T.qb[:, qcols(k)], T.sb[:, qcols(k)], True, True).then_inc(S["z0_%d" % k], 1)
+        if k == 0:
+            te.wait_ge(S.qa1, 1)
+        te.matmul_mx(T.z[:, bank(b1)], T.qa[:, qcols(1)], T.sa[:, qcols(1)],
+                     T.qb[:, qcols(k)], T.sb[:, qcols(k)], True, True).then_inc(S["z1_%d" % k], 1)
+        v.wait_ge(S["z0_%d" % k], 1)
+        v.tensor_scalar(T.gt[:, col(k, 0)], T.z[:, bank(b0)], 0.0, C,
+                        AluOpType.max, AluOpType.mult).then_inc(S["av%d" % k], 1)
+        v.tensor_scalar(T.gt[:, col(k, 1)], T.z[:, bank(b0)], -C, 0.0,
+                        AluOpType.mult, AluOpType.max).then_inc(S["av%d" % k], 1)
+        sc.wait_ge(S["z1_%d" % k], 1)
+        sc.activation(T.gt[:, col(k, 2)], T.z[:, bank(b1)], ActivationFunctionType.Relu,
+                      scale=C).then_inc(S["as%d" % k], 1)
+        sc.activation(T.gt[:, col(k, 3)], T.z[:, bank(b1)], ActivationFunctionType.Relu,
+                      scale=-C).then_inc(S["as%d" % k], 1)
+        v.wait_ge(S["av%d" % k], 2)
+        v.wait_ge(S["as%d" % k], 2)
+        v.quantize_mx(T.qg[:, qcols(k)], T.sg[:, qcols(k)], T.gt[:, tcols(k)]).then_inc(S["qg%d" % k], 1)
+        if k < 2:
+            dst = T.cores[order[k]]
+            rid, pid, _ = topo.addr(dst)
+            allowed = topo.mask(core, dst)
+            bits = [1 << e for e in range(16) if (allowed >> e) & 1]
+            halves = [sum(bits[0::2]), sum(bits[1::2])]
+            g.wait_ge(S["qg%d" % k], 1)
+            g.remote_dma(T["lq%d" % k][:, :].bitcast(dt.uint8), T.qg[:, qcols(k)].bitcast(dt.uint8),
+                         S["arr%d" % k], S.sent, pid, rid, halves[k])
+            g.remote_dma(T["ls%d" % k][:, :], T.sg[:, qcols(k)],
+                         S["arr%d" % k], S.sent, pid, rid, halves[1 - k])
+        if k == 1:
+            v.wait_ge(S.eye, 1)
+            for b in range(4):
+                v.quantize_mx(T.qs[:, qcols(b)], T.ss[:, qcols(b)],
+                              T.strip[:, 3 - b:3 - b + W]).then_inc(S.qs, 1)
+        if k < 2:
+            v.wait_ge(S["ld_b%d" % (k + 1)], 16)
+            v.quantize_mx(T.qb[:, qcols(k + 1)], T.sb[:, qcols(k + 1)],
+                          T.bt[:, tcols(k + 1)]).then_inc(S["qb%d" % (k + 1)], 1)
+
+    per_call = len(bits) // 2
+    g.wait_ge(S.sent, 4 * per_call)
+
+    seq = (0, 2, 1, 3)
+    te.wait_ge(S.qs, 4)
+    te.wait_ge(S.qg2, 1)
+    for b in seq:
+        te.matmul_mx(T.d[:, bank(b)], T.qs[:, qcols(b)], T.ss[:, qcols(b)],
+                     T.qg[:, qcols(2)], T.sg[:, qcols(2)], True, False)
+    te.wait_ge(S.arr0, 2 * per_call)
+    for b in seq:
+        te.matmul_mx(T.d[:, bank(b)], T.qs[:, qcols(b)], T.ss[:, qcols(b)],
+                     T.lq0[:, :], T.ls0[:, :], False, False)
+    te.wait_ge(S.arr1, 2 * per_call)
+    for b in seq:
+        te.matmul_mx(T.d[:, bank(b)], T.qs[:, qcols(b)], T.ss[:, qcols(b)],
+                     T.lq1[:, :], T.ls1[:, :], False, True).then_inc(S["dd%d" % b], 1)
+    for b in (0, 1):
+        v.wait_ge(S["dd%d" % b], 1)
+        v.tensor_copy(T.yt[:, b:W:4], T.d[:, bank(b)]).then_inc(S.yr, 1)
+    for b in (2, 3):
+        sc.wait_ge(S["dd%d" % b], 1)
+        sc.activation(T.yt[:, b:W:4], T.d[:, bank(b)], ActivationFunctionType.Copy).then_inc(S.yr, 1)
+    sy.wait_ge(S.yr, 4)
+    sy.dma_start(T.y[:, :], T.yt[:, :]).then_inc(S.st, 16)
+    sy.wait_ge(S.st, 16)

@@ -14,9 +14,12 @@ SCRATCH = {
     "gt": ("sbuf", [128, 3 * W], "bfloat16"),
     "qg": ("sbuf", [128, 3 * NC], "float8_e4m3fn_x4"),
     "sg": ("sbuf", [128, 3 * NC], "uint8"),
+    "idx": ("sbuf", [128, NC], "bfloat16"),
     "strip": ("sbuf", [128, W + 4], "bfloat16"),
     "qs": ("sbuf", [128, 4 * NC], "float8_e4m3fn_x4"),
     "ss": ("sbuf", [128, 4 * NC], "uint8"),
+    "lqs": ("sbuf", [128, NC], "float8_e4m3fn_x4"),
+    "lss": ("sbuf", [128, NC], "uint8"),
     "lq0": ("sbuf", [128, NC], "float8_e4m3fn_x4"),
     "ls0": ("sbuf", [128, NC], "uint8"),
     "lq1": ("sbuf", [128, NC], "float8_e4m3fn_x4"),
@@ -25,7 +28,7 @@ SCRATCH = {
     "z": ("psum", [128, 4 * 512], "float32"),
     "d": ("psum", [128, 4 * 512], "float32"),
 }
-SEMAPHORES = (["ld_a", "ones", "eye", "qa0", "qa1", "qs", "arr0", "arr1", "sent", "yr", "st"]
+SEMAPHORES = (["ld_a", "zero", "ramp", "eye", "qa0", "qa1", "qs1", "qs", "arrs", "arr0", "arr1", "sent", "yr", "st"]
               + ["%s%d" % (n, k) for n in ("ld_b", "qb", "z0_", "z1_", "av", "as", "qg") for k in range(3)]
               + ["dd%d" % b for b in range(4)])
 
@@ -48,14 +51,39 @@ def rank_program(g, core, T, topo):
     def bank(i):
         return slice(512 * i, 512 * i + NC)
 
+    def route(dst):
+        rid, pid, _ = topo.addr(dst)
+        allowed = topo.mask(core, dst)
+        bits = [1 << e for e in range(16) if (allowed >> e) & 1]
+        return rid, pid, [sum(bits[0::2]), sum(bits[1::2])], len(bits) // 2
+
+    def quantise_s(b, sem):
+        v.quantize_mx(T.qs[:, qcols(b)], T.ss[:, qcols(b)], T.strip[:, 3 - b:3 - b + W]).then_inc(sem, 1)
+
+    def s_tile(b):
+        if b == rank:
+            return T.lqs[:, :], T.lss[:, :]
+        return T.qs[:, qcols(b)], T.ss[:, qcols(b)]
+
     sy.dma_start(T.at[:, :], T.a[:, :]).then_inc(S.ld_a, 16)
     sc.dma_start(T.bt[:, tcols(0)], T.b[:, tcols(order[0])]).then_inc(S.ld_b0, 16)
     sy.dma_start(T.bt[:, tcols(1)], T.b[:, tcols(order[1])]).then_inc(S.ld_b1, 16)
     sc.dma_start(T.bt[:, tcols(2)], T.b[:, tcols(order[2])]).then_inc(S.ld_b2, 16)
 
-    v.memset(T.strip[:, :], 1.0).then_inc(S.ones, 1)
-    g.wait_ge(S.ones, 1)
-    g.affine_select(T.strip[:, :], T.strip[:, :], [[1, W + 4]], AluOpType.is_equal, 0.0, -3, -4).then_inc(S.eye, 1)
+    g.iota(T.idx[:, :], [[1, NC]], 0, -1, allow_small_or_imprecise_dtypes=True).then_inc(S.ramp, 1)
+    v.memset(T.strip[:, :], 0.0).then_inc(S.zero, 1)
+    v.wait_ge(S.zero, 1)
+    v.wait_ge(S.ramp, 1)
+    v.tensor_scalar(T.strip[:, 3:W + 3:4], T.idx[:, :], 0.0, None, AluOpType.is_equal).then_inc(S.eye, 1)
+    v.wait_ge(S.eye, 1)
+    quantise_s(order[0], S.qs1)
+    rid, pid, halves, per_call = route(T.cores[order[0]])
+    g.wait_ge(S.qs1, 1)
+    g.remote_dma(T.lqs[:, :].bitcast(dt.uint8), T.qs[:, qcols(order[0])].bitcast(dt.uint8),
+                 S.arrs, S.sent, pid, rid, halves[0])
+    g.remote_dma(T.lss[:, :], T.ss[:, qcols(order[0])], S.arrs, S.sent, pid, rid, halves[1])
+    quantise_s(order[1], S.qs)
+    quantise_s(3, S.qs)
 
     v.wait_ge(S.ld_b0, 16)
     v.quantize_mx(T.qb[:, qcols(0)], T.sb[:, qcols(0)], T.bt[:, tcols(0)]).then_inc(S.qb0, 1)
@@ -92,47 +120,40 @@ def rank_program(g, core, T, topo):
                       scale=C).then_inc(S["as%d" % k], 1)
         sc.activation(T.gt[:, col(k, 3)], T.z[:, bank(b1)], ActivationFunctionType.Relu,
                       scale=-C).then_inc(S["as%d" % k], 1)
+        if k < 2:
+            v.wait_ge(S["ld_b%d" % (k + 1)], 16)
+            v.quantize_mx(T.qb[:, qcols(k + 1)], T.sb[:, qcols(k + 1)],
+                          T.bt[:, tcols(k + 1)]).then_inc(S["qb%d" % (k + 1)], 1)
         v.wait_ge(S["av%d" % k], 2)
         v.wait_ge(S["as%d" % k], 2)
         v.quantize_mx(T.qg[:, qcols(k)], T.sg[:, qcols(k)], T.gt[:, tcols(k)]).then_inc(S["qg%d" % k], 1)
         if k < 2:
-            dst = T.cores[order[k]]
-            rid, pid, _ = topo.addr(dst)
-            allowed = topo.mask(core, dst)
-            bits = [1 << e for e in range(16) if (allowed >> e) & 1]
-            halves = [sum(bits[0::2]), sum(bits[1::2])]
+            rid, pid, halves, per_call = route(T.cores[order[k]])
             g.wait_ge(S["qg%d" % k], 1)
             g.remote_dma(T["lq%d" % k][:, :].bitcast(dt.uint8), T.qg[:, qcols(k)].bitcast(dt.uint8),
                          S["arr%d" % k], S.sent, pid, rid, halves[k])
             g.remote_dma(T["ls%d" % k][:, :], T.sg[:, qcols(k)],
                          S["arr%d" % k], S.sent, pid, rid, halves[1 - k])
-        if k == 1:
-            v.wait_ge(S.eye, 1)
-            for b in range(4):
-                v.quantize_mx(T.qs[:, qcols(b)], T.ss[:, qcols(b)],
-                              T.strip[:, 3 - b:3 - b + W]).then_inc(S.qs, 1)
-        if k < 2:
-            v.wait_ge(S["ld_b%d" % (k + 1)], 16)
-            v.quantize_mx(T.qb[:, qcols(k + 1)], T.sb[:, qcols(k + 1)],
-                          T.bt[:, tcols(k + 1)]).then_inc(S["qb%d" % (k + 1)], 1)
 
-    per_call = len(bits) // 2
-    g.wait_ge(S.sent, 4 * per_call)
+    g.wait_ge(S.sent, 6 * per_call)
 
-    seq = (0, 2, 1, 3)
-    te.wait_ge(S.qs, 4)
+    te.wait_ge(S.qs1, 1)
+    te.wait_ge(S.qs, 2)
     te.wait_ge(S.qg2, 1)
-    for b in seq:
-        te.matmul_mx(T.d[:, bank(b)], T.qs[:, qcols(b)], T.ss[:, qcols(b)],
-                     T.qg[:, qcols(2)], T.sg[:, qcols(2)], True, False)
+    for b in [x for x in range(4) if x != rank] + [rank]:
+        if b == rank:
+            te.wait_ge(S.arrs, 2 * per_call)
+        cs, ps = s_tile(b)
+        te.matmul_mx(T.d[:, bank(b)], cs, ps, T.qg[:, qcols(2)], T.sg[:, qcols(2)], True, False)
+    seq = (0, 2, 1, 3)
     te.wait_ge(S.arr0, 2 * per_call)
     for b in seq:
-        te.matmul_mx(T.d[:, bank(b)], T.qs[:, qcols(b)], T.ss[:, qcols(b)],
-                     T.lq0[:, :], T.ls0[:, :], False, False)
+        cs, ps = s_tile(b)
+        te.matmul_mx(T.d[:, bank(b)], cs, ps, T.lq0[:, :], T.ls0[:, :], False, False)
     te.wait_ge(S.arr1, 2 * per_call)
     for b in seq:
-        te.matmul_mx(T.d[:, bank(b)], T.qs[:, qcols(b)], T.ss[:, qcols(b)],
-                     T.lq1[:, :], T.ls1[:, :], False, True).then_inc(S["dd%d" % b], 1)
+        cs, ps = s_tile(b)
+        te.matmul_mx(T.d[:, bank(b)], cs, ps, T.lq1[:, :], T.ls1[:, :], False, True).then_inc(S["dd%d" % b], 1)
     for b in (0, 1):
         v.wait_ge(S["dd%d" % b], 1)
         v.tensor_copy(T.yt[:, b:W:4], T.d[:, bank(b)]).then_inc(S.yr, 1)

from concourse.mybir import dt, AluOpType, ActivationFunctionType

C = 0.037
W = 512
NC = 128

SCRATCH = {
    "at": ("sbuf", [128, 2 * W], "bfloat16"),
    "bt": ("sbuf", [128, 3 * W], "bfloat16"),
    "qa": ("sbuf", [128, 2 * NC], "float8_e4m3fn_x4"),
    "sa": ("sbuf", [128, 2 * NC], "uint8"),
    "qb": ("sbuf", [128, 3 * NC], "float8_e4m3fn_x4"),
    "sb": ("sbuf", [128, 3 * NC], "uint8"),
    "gt": ("sbuf", [128, 3 * W], "bfloat16"),
    "qg": ("sbuf", [128, 3 * NC], "float8_e4m3fn_x4"),
    "sg": ("sbuf", [128, 3 * NC], "uint8"),
    "idx": ("sbuf", [128, NC], "bfloat16"),
    "strip": ("sbuf", [128, W + 4], "bfloat16"),
    "qs": ("sbuf", [128, 4 * NC], "float8_e4m3fn_x4"),
    "ss": ("sbuf", [128, 4 * NC], "uint8"),
    "lqs": ("sbuf", [128, NC], "float8_e4m3fn_x4"),
    "lss": ("sbuf", [128, NC], "uint8"),
    "lq0": ("sbuf", [128, NC], "float8_e4m3fn_x4"),
    "ls0": ("sbuf", [128, NC], "uint8"),
    "lq1": ("sbuf", [128, NC], "float8_e4m3fn_x4"),
    "ls1": ("sbuf", [128, NC], "uint8"),
    "yt": ("sbuf", [128, W], "float32"),
    "z": ("psum", [128, 4 * 512], "float32"),
    "d": ("psum", [128, 4 * 512], "float32"),
}
SEMAPHORES = (["ld_a", "zero", "ramp", "eye", "qa0", "qa1", "qs1", "qs", "arrs", "arr0", "arr1", "sent", "yr", "st"]
              + ["%s%d" % (n, k) for n in ("ld_b", "qb", "z0_", "z1_", "av", "as", "qg") for k in range(3)]
              + ["dd%d" % b for b in range(4)])


def rank_program(g, core, T, topo):
    rank = T.rank_of(core)
    if rank is None:
        return
    n = len(T.cores)
    S = T.sem
    v, sc, te, sy = g.vector, g.scalar, g.tensor, g.sync
    order = [(rank + 1) % n, (rank + 2) % n, rank]

    def tcols(i):
        return slice(W * i, W * i + W)

    def qcols(i):
        return slice(NC * i, NC * i + NC)

    def bank(i):
        return slice(512 * i, 512 * i + NC)

    def route(dst):
        rid, pid, _ = topo.addr(dst)
        allowed = topo.mask(core, dst)
        bits = [1 << e for e in range(16) if (allowed >> e) & 1]
        return rid, pid, [sum(bits[0::2]), sum(bits[1::2])], len(bits) // 2

    def quantise_s(b, sem):
        v.quantize_mx(T.qs[:, qcols(b)], T.ss[:, qcols(b)], T.strip[:, 3 - b:3 - b + W]).then_inc(sem, 1)

    def s_tile(b):
        if b == rank:
            return T.lqs[:, :], T.lss[:, :]
        return T.qs[:, qcols(b)], T.ss[:, qcols(b)]

    sy.dma_start(T.at[:, :], T.a[:, :]).then_inc(S.ld_a, 16)
    sc.dma_start(T.bt[:, tcols(0)], T.b[:, tcols(order[0])]).then_inc(S.ld_b0, 16)
    sy.dma_start(T.bt[:, tcols(1)], T.b[:, tcols(order[1])]).then_inc(S.ld_b1, 16)
    sc.dma_start(T.bt[:, tcols(2)], T.b[:, tcols(order[2])]).then_inc(S.ld_b2, 16)

    g.iota(T.idx[:, :], [[1, NC]], 0, -1, allow_small_or_imprecise_dtypes=True).then_inc(S.ramp, 1)
    v.memset(T.strip[:, :], 0.0).then_inc(S.zero, 1)
    v.wait_ge(S.zero, 1)
    v.wait_ge(S.ramp, 1)
    v.tensor_scalar(T.strip[:, 3:W + 3:4], T.idx[:, :], 0.0, None, AluOpType.is_equal).then_inc(S.eye, 1)
    v.wait_ge(S.eye, 1)
    quantise_s(order[0], S.qs1)
    rid, pid, halves, per_call = route(T.cores[order[0]])
    g.wait_ge(S.qs1, 1)
    g.remote_dma(T.lqs[:, :].bitcast(dt.uint8), T.qs[:, qcols(order[0])].bitcast(dt.uint8),
                 S.arrs, S.sent, pid, rid, halves[0])
    g.remote_dma(T.lss[:, :], T.ss[:, qcols(order[0])], S.arrs, S.sent, pid, rid, halves[1])
    quantise_s(order[1], S.qs)
    quantise_s(3, S.qs)

    v.wait_ge(S.ld_b0, 16)
    v.quantize_mx(T.qb[:, qcols(0)], T.sb[:, qcols(0)], T.bt[:, tcols(0)]).then_inc(S.qb0, 1)
    v.wait_ge(S.ld_a, 16)
    for i in range(2):
        v.quantize_mx(T.qa[:, qcols(i)], T.sa[:, qcols(i)], T.at[:, tcols(i)]).then_inc(S["qa%d" % i], 1)

    zbank = [(0, 1), (2, 3), (0, 1)]

    def col(k, b):
        return slice(W * k + b, W * k + W, 4)

    for k in range(3):
        b0, b1 = zbank[k]
        te.wait_ge(S["qb%d" % k], 1)
        if k == 0:
            te.wait_ge(S.qa0, 1)
        if k == 2:
            te.wait_ge(S.av0, 2)
            te.wait_ge(S.as0, 2)
        te.matmul_mx(T.z[:, bank(b0)], T.qa[:, qcols(0)], T.sa[:, qcols(0)],
                     T.qb[:, qcols(k)], T.sb[:, qcols(k)], True, True).then_inc(S["z0_%d" % k], 1)
        if k == 0:
            te.wait_ge(S.qa1, 1)
        te.matmul_mx(T.z[:, bank(b1)], T.qa[:, qcols(1)], T.sa[:, qcols(1)],
                     T.qb[:, qcols(k)], T.sb[:, qcols(k)], True, True).then_inc(S["z1_%d" % k], 1)
        v.wait_ge(S["z0_%d" % k], 1)
        v.tensor_scalar(T.gt[:, col(k, 0)], T.z[:, bank(b0)], 0.0, C,
                        AluOpType.max, AluOpType.mult).then_inc(S["av%d" % k], 1)
        v.tensor_scalar(T.gt[:, col(k, 1)], T.z[:, bank(b0)], -C, 0.0,
                        AluOpType.mult, AluOpType.max).then_inc(S["av%d" % k], 1)
        sc.wait_ge(S["z1_%d" % k], 1)
        sc.activation(T.gt[:, col(k, 2)], T.z[:, bank(b1)], ActivationFunctionType.Relu,
                      scale=C).then_inc(S["as%d" % k], 1)
        sc.activation(T.gt[:, col(k, 3)], T.z[:, bank(b1)], ActivationFunctionType.Relu,
                      scale=-C).then_inc(S["as%d" % k], 1)
        if k < 2:
            v.wait_ge(S["ld_b%d" % (k + 1)], 16)
            v.quantize_mx(T.qb[:, qcols(k + 1)], T.sb[:, qcols(k + 1)],
                          T.bt[:, tcols(k + 1)]).then_inc(S["qb%d" % (k + 1)], 1)
        v.wait_ge(S["av%d" % k], 2)
        v.wait_ge(S["as%d" % k], 2)
        v.quantize_mx(T.qg[:, qcols(k)], T.sg[:, qcols(k)], T.gt[:, tcols(k)]).then_inc(S["qg%d" % k], 1)
        if k < 2:
            rid, pid, halves, per_call = route(T.cores[order[k]])
            g.wait_ge(S["qg%d" % k], 1)
            g.remote_dma(T["lq%d" % k][:, :].bitcast(dt.uint8), T.qg[:, qcols(k)].bitcast(dt.uint8),
                         S["arr%d" % k], S.sent, pid, rid, halves[k])
            g.remote_dma(T["ls%d" % k][:, :], T.sg[:, qcols(k)],
                         S["arr%d" % k], S.sent, pid, rid, halves[1 - k])

    g.wait_ge(S.sent, 6 * per_call)

    te.wait_ge(S.qs1, 1)
    te.wait_ge(S.qs, 2)
    te.wait_ge(S.qg2, 1)
    for b in [x for x in range(4) if x != rank] + [rank]:
        if b == rank:
            te.wait_ge(S.arrs, 2 * per_call)
        cs, ps = s_tile(b)
        te.matmul_mx(T.d[:, bank(b)], cs, ps, T.qg[:, qcols(2)], T.sg[:, qcols(2)], True, False)
    seq = (0, 2, 1, 3)
    te.wait_ge(S.arr0, 2 * per_call)
    for b in seq:
        cs, ps = s_tile(b)
        te.matmul_mx(T.d[:, bank(b)], cs, ps, T.lq0[:, :], T.ls0[:, :], False, False)
    te.wait_ge(S.arr1, 2 * per_call)
    for b in seq:
        cs, ps = s_tile(b)
        te.matmul_mx(T.d[:, bank(b)], cs, ps, T.lq1[:, :], T.ls1[:, :], False, True).then_inc(S["dd%d" % b], 1)
    for b in (0, 1):
        v.wait_ge(S["dd%d" % b], 1)
        v.tensor_copy(T.yt[:, b:W:4], T.d[:, bank(b)]).then_inc(S.yr, 1)
    for b in (2, 3):
        sc.wait_ge(S["dd%d" % b], 1)
        sc.activation(T.yt[:, b:W:4], T.d[:, bank(b)], ActivationFunctionType.Copy).then_inc(S.yr, 1)
    sy.wait_ge(S.yr, 4)
    sy.dma_start(T.y[:, :], T.yt[:, :]).then_inc(S.st, 16)
    sy.wait_ge(S.st, 16)
